import numpy as np
import ml_dtypes


def mxq(x, axis, fmt="e4m3"):
    dtype, down = {"e4m3": (ml_dtypes.float8_e4m3fn, 7), "e5m2": (ml_dtypes.float8_e5m2, 14)}[fmt]
    v = np.moveaxis(np.asarray(x, np.float32).astype(ml_dtypes.bfloat16).astype(np.float64), axis, -1)
    blocks = v.reshape(v.shape[:-1] + (-1, 32))
    amax = np.abs(blocks).max(-1, keepdims=True)
    byte = np.maximum(np.where(amax > 0, np.frexp(amax)[1] - 1 + 127, 0) - down, 1)
    scale = np.exp2(byte - 127.0)
    codes = (blocks / scale).astype(np.float32).astype(dtype).astype(np.float64)
    return np.moveaxis((codes * scale).reshape(v.shape), -1, axis)


WIDE = False


def mx_kscale(k):
    if not WIDE:
        return np.ones(k)
    levels = np.array([30, -30])
    if k % 512:
        return np.exp2(np.random.permutation(np.resize(levels, k // 32))).repeat(32)
    a = np.empty((k // 512, 16))
    for p in range(k // 512):
        a[p, :8] = np.random.permutation(np.resize(levels, 8))
        for g in range(8):
            far = levels[np.abs(levels - a[p, g]) >= 10]
            a[p, g + 8] = far[np.random.randint(len(far))]
    return np.exp2(a.ravel()).repeat(32)


BF16 = ml_dtypes.bfloat16


def bf(x):
    return np.asarray(x, np.float32).astype(BF16)


def f64(x):
    return np.asarray(x).astype(np.float64)


E2M1 = np.array([0.0, 0.5, 1.0, 1.5, 2.0, 3.0, 4.0, 6.0, -0.0, -0.5, -1.0, -1.5, -2.0, -3.0, -4.0, -6.0])


def pack_weight(w, fmt):
    k, n = w.shape
    w = f64(bf(w)).reshape(k // 32, 32, n)
    amax = np.abs(w).max(1)
    if fmt in ("e4m3", "e5m2"):
        byte = np.frexp(amax)[1] - 1 + 127 - (7 if fmt == "e4m3" else 14)
    else:
        mant, ex = np.frexp(amax / 6.0)
        byte = np.where(mant > 0.5, ex, ex - 1) + 127
    byte = np.clip(np.where(amax > 0, byte, 1), 1, 254)
    scaled = (w * np.exp2(127.0 - byte)[:, None, :]).reshape(k, n).astype(np.float32)
    by_word = np.ascontiguousarray(scaled.reshape(k // 512, 128, 4, n).transpose(0, 1, 3, 2))
    if fmt in ("e4m3", "e5m2"):
        words = by_word.astype(ml_dtypes.float8_e4m3fn if fmt == "e4m3" else ml_dtypes.float8_e5m2).view(np.uint8)
    else:
        c = by_word.astype(ml_dtypes.float4_e2m1fn).view(np.uint8) & 0xF
        words = c[..., 0::2] | (c[..., 1::2] << 4)
    return np.ascontiguousarray(words), np.ascontiguousarray(byte.astype(np.uint8).reshape(k // 512, 16, n))


def unpack_weight(words, scales, fmt):
    g, p, n, _ = words.shape
    if fmt in ("e4m3", "e5m2"):
        vals = np.ascontiguousarray(words).view(ml_dtypes.float8_e4m3fn if fmt == "e4m3" else ml_dtypes.float8_e5m2).astype(np.float64)
    else:
        nib = np.empty((g, p, n, 4), np.uint8)
        nib[..., 0::2] = words & 0xF
        nib[..., 1::2] = words >> 4
        vals = E2M1[nib]
    vals = vals * np.repeat(np.exp2(scales.astype(np.float64) - 127.0), 8, axis=1)[..., None]
    return vals.transpose(0, 1, 3, 2).reshape(g * 512, n)


I, T, P, K, R = 4, 1024, 256, 1024, 1024


def setup_inputs():
    s = mx_kscale(K)
    r = mx_kscale(R)
    G = np.random.standard_t(5, (K, I * T)) * s[:, None]
    g_words, g_scales = pack_weight(G, "e5m2")
    return {"g_words": g_words,
            "g_scales": g_scales,
            "w": bf(np.random.standard_normal((I, P, K)) / np.sqrt(K) / s),
            "e": bf(np.random.standard_normal((T, R)) * r),
            "d": bf(np.random.standard_normal((I, P, R)) / np.sqrt(R) / r),
            "gate": bf(1 + 0.25 * np.random.standard_normal((I, T)))}


def reference(g_words, g_scales, w, e, d, gate):
    gv = unpack_weight(g_words, g_scales, "e5m2").reshape(K, I, T).transpose(1, 2, 0)
    wq = mxq(f64(w), 2, "e4m3").transpose(0, 2, 1)
    eq = mxq(f64(e), 1, "e4m3")
    dq = mxq(f64(d), 2, "e4m3").transpose(0, 2, 1)
    votes = gv @ wq
    recon = eq @ dq
    du = votes + recon
    return du * f64(gate)[:, :, None]

@@ -1,0 +1,250 @@
+from contextlib import ExitStack
+
+import concourse.mybir as mybir
+from concourse.masks import make_identity
+
+F32 = mybir.dt.float32
+BF16 = mybir.dt.bfloat16
+U32 = mybir.dt.uint32
+I32 = mybir.dt.int32
+U8 = mybir.dt.uint8
+E4M3X4 = mybir.dt.float8_e4m3fn_x4
+E5M2X4 = mybir.dt.float8_e5m2_x4
+COPY = mybir.ActivationFunctionType.Copy
+MULT = mybir.AluOpType.mult
+
+TYPES, TOKENS, POSE, K = 4, 1024, 256, 1024
+P = 128
+G = K // 512
+
+FLOPS = 2 * TYPES * TOKENS * POSE * (K + K)
+BYTES = 2 * 128 * 4096 * 4 + 2 * 16 * 4096 + 3 * 2 * 1024 * 1024 + 2 * 4096 + 4 * 4096 * 256
+
+
+def tile_capsule_pose_gradient_e4_kernel(tc, g_words, g_scales, w, e, d, gate, out):
+    nc = tc.nc
+    with ExitStack() as ctx:
+        keep = ctx.enter_context(tc.tile_pool(name="keep", bufs=1))
+        stage = ctx.enter_context(tc.tile_pool(name="stage", bufs=3))
+        outs = ctx.enter_context(tc.tile_pool(name="outs", bufs=8))
+        xtp = ctx.enter_context(tc.psum_pool(name="xtp", bufs=4))
+        accp = ctx.enter_context(tc.psum_pool(name="accp", bufs=4))
+        ctx.enter_context(tc.manual_schedule())
+
+        raw = {}
+        for kind, n in (("w", 4), ("d", 4), ("e", 4)):
+            for b in range(n):
+                raw[kind, b] = keep.tile([P, 2, K], BF16, name="raw_%s%d" % (kind, b), align_bytes=64)
+        src = {"w": w.rearrange("i (p s) k -> i p s k", s=2),
+               "d": d.rearrange("i (p s) k -> i p s k", s=2),
+               "e": e.rearrange("(i p s) k -> i p s k", p=P, s=2)}
+        gw = {}
+        for i in range(TYPES):
+            for h in range(2):
+                gw[i, h] = keep.tile([P, G, 512], U32, name="gw_%d%d" % (i, h), align_bytes=64)
+        plane = [keep.tile([P, G, 2048], U8, name="plane_%d" % j, align_bytes=64) for j in range(2)]
+        wc = [keep.tile([P, G, 768], U32, name="wc_%d" % j, align_bytes=64) for j in range(2)]
+        ws = [keep.tile([P, G, 768], U8, name="ws_%d" % j, align_bytes=64) for j in range(2)]
+        dc = [keep.tile([P, G, 512], U32, name="dc_%d" % j, align_bytes=64) for j in range(2)]
+        ds = [keep.tile([P, G, 512], U8, name="ds_%d" % j, align_bytes=64) for j in range(2)]
+        ec = [keep.tile([P, G, 256], U32, name="ec_%d" % b, align_bytes=64) for b in range(4)]
+        es = [keep.tile([P, G, 256], U8, name="es_%d" % b, align_bytes=64) for b in range(4)]
+        ident = keep.tile([P, P], F32, name="ident")
+        gate_bf = keep.tile([32, P], BF16, name="gate_bf")
+        gate_f = keep.tile([P, P], F32, name="gate_f")
+        gate_t = keep.tile([P, 32], F32, name="gate_t")
+        warm = keep.tile([P, 1], F32, name="warm")
+
+        def load(kind, b):
+            nc.sync.dma_start(out=raw[kind, b][:], in_=src[kind][b])
+
+        def load_halves(kind, b):
+            for g in range(G):
+                ks = slice(512 * g, 512 * (g + 1))
+                nc.sync.dma_start(out=raw[kind, b][:, :, ks], in_=src[kind][b][:, :, ks])
+
+        def load_g(i, h):
+            n0 = TOKENS * i + 512 * h
+            for g in range(G):
+                nc.sync.dma_start(out=gw[i, h][:, g, :].bitcast(I32),
+                                  in_=g_words[g, :, n0:n0 + 512, :].rearrange("p n t -> p (n t)").bitcast(I32))
+
+        def load_scales(j):
+            for q in range(4):
+                nc.sync.dma_start(
+                    out=plane[j][32 * q:32 * q + 4, :, :].bitcast(I32),
+                    in_=g_scales[:, 4 * q:4 * q + 4, 2048 * j:2048 * (j + 1)].rearrange("g q n -> q g n").bitcast(I32))
+
+        nc.vector.memset(plane[0][:].bitcast(I32), 0)
+        nc.vector.memset(plane[1][:].bitcast(I32), 0)
+        nc.vector.memset(gate_f[:], 0.0)
+        nc.vector.memset(warm[:], 0.0)
+        nc.scalar.activation(out=warm[:], in_=warm[:], func=COPY, scale=1.0)
+        make_identity(nc, ident[:])
+        for j in range(2):
+            nc.gpsimd.memset(wc[j][:, :, 256:512], 0)
+            nc.gpsimd.memset(ws[j][:].bitcast(I32)[:, :, 64:128], 0)
+        load_halves("w", 0)
+        load_scales(0)
+        load_g(0, 0)
+        load("w", 1)
+        load("e", 0)
+        load("d", 0)
+        load("d", 1)
+        nc.sync.dma_start(out=gate_bf[:], in_=gate.rearrange("i (t p) -> (i t) p", p=P))
+        load_g(1, 0)
+        load("e", 1)
+        load_g(0, 1)
+        load_g(1, 1)
+        load("e", 2)
+        load("e", 3)
+        load("w", 2)
+        load("w", 3)
+        load_scales(1)
+        load("d", 2)
+        load("d", 3)
+        for i, h in ((2, 0), (3, 0), (2, 1), (3, 1)):
+            load_g(i, h)
+
+        ordered = {}
+
+        def reorder(kind, b):
+            t = stage.tile([P, 2, G, 2, P], F32, name="ordered", align_bytes=64)
+            nc.vector.tensor_copy(
+                out=t[:].rearrange("p s g u m -> p (s g) u m"),
+                in_=raw[kind, b][:].rearrange("p s k -> p (s k)").bitcast(F32).rearrange(
+                    "p (s m u) -> p s u m", s=4, u=2))
+            ordered[kind, b] = t
+
+        banks_of = {}
+
+        def turn(kind, b):
+            banks = []
+            for g in range(G):
+                xt = xtp.tile([P, 2, 2, P], F32, name="xt")
+                for s in range(2):
+                    for u in range(2):
+                        if (kind, b) in ordered:
+                            words = ordered[kind, b][:, s, g, u, :]
+                        else:
+                            words = raw[kind, b][:, s, :].bitcast(F32)[:, 256 * g + u:256 * (g + 1):2]
+                        nc.tensor.transpose(xt[:, s, u, :], words, ident[:])
+                banks.append(xt)
+            banks_of[kind, b] = banks
+
+        def quantise(kind, b, engines):
+            banks = banks_of[kind, b]
+            grouped = []
+            for g in range(G):
+                t = stage.tile([P, 1024], BF16, name="grouped%d" % g, align_bytes=64)
+                dst = t[:].bitcast(F32).rearrange("p (r s u) -> p r s u", s=2, u=2)
+                view = banks[g][:].rearrange("p s u r -> p r s u")
+                if engines[g] == "s":
+                    nc.scalar.copy(out=dst, in_=view)
+                else:
+                    nc.vector.tensor_copy(out=dst, in_=view)
+                grouped.append(t)
+            for g in range(G):
+                if kind == "w":
+                    c0 = 512 * (b % 2)
+                    codes, scales = wc[b // 2][:, g, c0:c0 + 256], ws[b // 2][:, g, c0:c0 + 256]
+                elif kind == "d":
+                    c0 = 256 * (b % 2)
+                    codes, scales = dc[b // 2][:, g, c0:c0 + 256], ds[b // 2][:, g, c0:c0 + 256]
+                else:
+                    codes, scales = ec[b][:, g, :], es[b][:, g, :]
+                nc.vector.quantize_mx(out=codes.bitcast(E4M3X4), scales=scales, in_=grouped[g][:])
+
+        acc = {}
+
+        def votes(i, tt):
+            j, h = i // 2, i % 2
+            if h == 0:
+                acc[j, tt] = accp.tile([P, 512], F32, name="acc")
+            cols = slice(128 * (tt % 4), 128 * (tt % 4) + 128)
+            n0 = TOKENS * h + 128 * tt
+            mov = slice(256 * h, 256 * h + 512)
+            for g in range(G):
+                nc.tensor.matmul_mx(
+                    out=acc[j, tt][:],
+                    lhsT=gw[i, tt // 4][:, g, cols].bitcast(E5M2X4),
+                    lhsT_scale=plane[j][:, g, n0:n0 + 128],
+                    rhs=wc[j][:, g, mov].bitcast(E4M3X4), rhs_scale=ws[j][:, g, mov],
+                    start=(h == 0 and g == 0), stop=False)
+
+        def recon(j, tt):
+            cols = slice(128 * (tt % 2), 128 * (tt % 2) + 128)
+            for g in range(G):
+                nc.tensor.matmul_mx(
+                    out=acc[j, tt][:],
+                    lhsT=ec[tt // 2][:, g, cols].bitcast(E4M3X4), lhsT_scale=es[tt // 2][:, g, cols],
+                    rhs=dc[j][:, g, :].bitcast(E4M3X4), rhs_scale=ds[j][:, g, :],
+                    start=False, stop=(g == G - 1))
+
+        def finish(j, tt, vector):
+            ob = outs.tile([P, 2, POSE], F32, name="ob")
+            for h in range(2):
+                c = (2 * j + h) * 8 + tt
+                part = acc[j, tt][:, POSE * h:POSE * (h + 1)]
+                if vector:
+                    nc.vector.tensor_scalar(out=ob[:, h, :], in0=part, scalar1=gate_t[:, c:c + 1], scalar2=None, op0=MULT)
+                else:
+                    nc.scalar.activation(out=ob[:, h, :], in_=part, func=COPY, scale=gate_t[:, c:c + 1])
+            nc.sync.dma_start(
+                out=out[2 * j:2 * j + 2, P * tt:P * (tt + 1), :].rearrange("h p c -> p h c"), in_=ob[:])
+
+        def prep_gate():
+            nc.vector.tensor_copy(out=gate_f[0:32, :], in_=gate_bf[:])
+            gt = xtp.tile([P, 2, 2, P], F32, name="xt")
+            nc.tensor.transpose(gt[:, 0, 0, :], gate_f[:], ident[:])
+            nc.vector.tensor_copy(out=gate_t[:], in_=gt[:, 0, 0, 0:32])
+
+        def run_votes(i, tts):
+            for tt in tts:
+                votes(i, tt)
+
+        def run_recon(j, tts, vector):
+            for tt in tts:
+                recon(j, tt)
+                finish(j, tt, vector)
+
+        turn("w", 0)
+        quantise("w", 0, "sv")
+        run_votes(0, (0, 1, 2, 3))
+        reorder("e", 0)
+        reorder("d", 0)
+        turn("w", 1)
+        turn("e", 0)
+        quantise("w", 1, "ss")
+        reorder("d", 1)
+        turn("d", 0)
+        quantise("e", 0, "ss")
+        turn("d", 1)
+        quantise("d", 0, "ss")
+        reorder("e", 1)
+        quantise("d", 1, "vs")
+        run_votes(1, (0, 1))
+        turn("e", 1)
+        prep_gate()
+        quantise("e", 1, "sv")
+        run_votes(1, (2, 3))
+        reorder("e", 2)
+        run_recon(0, (0, 1), True)
+        reorder("e", 3)
+        run_recon(0, (2, 3), True)
+        for first, second, i, tts in (("e", "w", 0, (4, 5, 6, 7)), ("w", "d", 1, (4, 5, 6, 7))):
+            for b in (2, 3):
+                turn(first, b)
+                reorder(second, b)
+            for b in (2, 3):
+                quantise(first, b, "ss")
+            run_votes(i, tts)
+        for b in (2, 3):
+            turn("d", b)
+        for b in (2, 3):
+            quantise("d", b, "sv")
+        run_recon(0, (4, 5, 6, 7), False)
+        for tt in range(8):
+            votes(2, tt)
+            votes(3, tt)
+            run_recon(1, (tt,), tt % 2 == 0)

@@ -53,6 +53,9 @@ def tile_capsule_pose_gradient_e4_kernel(tc, g_words, g_scales, w, e, d, gate, o
         gate_bf = keep.tile([32, P], BF16, name="gate_bf")
         gate_f = keep.tile([P, P], F32, name="gate_f")
         gate_t = keep.tile([P, 32], F32, name="gate_t")
+        zeros = keep.tile([P, 2048], BF16, name="zeros", align_bytes=64)
+        zc = keep.tile([P, 512], U32, name="zc", align_bytes=64)
+        zs = keep.tile([P, 512], U8, name="zs", align_bytes=64)
         warm = keep.tile([P, 1], F32, name="warm")
 
         def load(kind, b):
@@ -65,34 +68,39 @@ def tile_capsule_pose_gradient_e4_kernel(tc, g_words, g_scales, w, e, d, gate, o
 
         def load_g(i, h):
             n0 = TOKENS * i + 512 * h
-            for g in range(G):
-                nc.sync.dma_start(out=gw[i, h][:, g, :].bitcast(I32),
-                                  in_=g_words[g, :, n0:n0 + 512, :].rearrange("p n t -> p (n t)").bitcast(I32))
+            nc.sync.dma_start(
+                out=gw[i, h][:].bitcast(I32),
+                in_=g_words.rearrange("g p n t -> p g (n t)")[:, :, 4 * n0:4 * (n0 + 512)].bitcast(I32))
 
-        def load_scales(j):
+        def load_scales(queue, j, c0, c1):
             for q in range(4):
-                nc.sync.dma_start(
-                    out=plane[j][32 * q:32 * q + 4, :, :].bitcast(I32),
-                    in_=g_scales[:, 4 * q:4 * q + 4, 2048 * j:2048 * (j + 1)].rearrange("g q n -> q g n").bitcast(I32))
+                queue.dma_start(
+                    out=plane[j][32 * q:32 * q + 4, :, c0:c1].bitcast(I32),
+                    in_=g_scales[:, 4 * q:4 * q + 4, 2048 * j + c0:2048 * j + c1].rearrange("g q n -> q g n").bitcast(I32))
 
-        nc.vector.memset(plane[0][:].bitcast(I32), 0)
-        nc.vector.memset(plane[1][:].bitcast(I32), 0)
-        nc.vector.memset(gate_f[:], 0.0)
+        planes32 = [plane[j][:].bitcast(I32) for j in range(2)]
+        nc.vector.memset(planes32[0][:, :, 0:128], 0)
+        nc.vector.memset(zeros[:].bitcast(I32), 0)
+        nc.vector.quantize_mx(out=zc[:].bitcast(E4M3X4), scales=zs[:], in_=zeros[:])
+        nc.vector.memset(planes32[0][:, :, 128:512], 0)
         nc.vector.memset(warm[:], 0.0)
-        nc.scalar.activation(out=warm[:], in_=warm[:], func=COPY, scale=1.0)
+        nc.vector.memset(gate_f[:], 0.0)
+        nc.vector.memset(planes32[1], 0)
         make_identity(nc, ident[:])
         for j in range(2):
             nc.gpsimd.memset(wc[j][:, :, 256:512], 0)
             nc.gpsimd.memset(ws[j][:].bitcast(I32)[:, :, 64:128], 0)
         load_halves("w", 0)
-        load_scales(0)
+        load_scales(nc.scalar, 0, 0, 512)
+        nc.scalar.activation(out=warm[:], in_=warm[:], func=COPY, scale=1.0)
         load_g(0, 0)
         load("w", 1)
         load("e", 0)
+        load_scales(nc.sync, 0, 512, 2048)
+        load_g(1, 0)
         load("d", 0)
         load("d", 1)
         nc.sync.dma_start(out=gate_bf[:], in_=gate.rearrange("i (t p) -> (i t) p", p=P))
-        load_g(1, 0)
         load("e", 1)
         load_g(0, 1)
         load_g(1, 1)
@@ -100,7 +108,7 @@ def tile_capsule_pose_gradient_e4_kernel(tc, g_words, g_scales, w, e, d, gate, o
         load("e", 3)
         load("w", 2)
         load("w", 3)
-        load_scales(1)
+        load_scales(nc.sync, 1, 0, 2048)
         load("d", 2)
         load("d", 3)
         for i, h in ((2, 0), (3, 0), (2, 1), (3, 1)):
@@ -190,8 +198,11 @@ def tile_capsule_pose_gradient_e4_kernel(tc, g_words, g_scales, w, e, d, gate, o
                     nc.vector.tensor_scalar(out=ob[:, h, :], in0=part, scalar1=gate_t[:, c:c + 1], scalar2=None, op0=MULT)
                 else:
                     nc.scalar.activation(out=ob[:, h, :], in_=part, func=COPY, scale=gate_t[:, c:c + 1])
-            nc.sync.dma_start(
-                out=out[2 * j:2 * j + 2, P * tt:P * (tt + 1), :].rearrange("h p c -> p h c"), in_=ob[:])
+                if (j, tt) == (1, 7):
+                    (nc.sync, nc.scalar)[h].dma_start(out=out[2 * j + h, P * tt:P * (tt + 1), :], in_=ob[:, h, :])
+            if (j, tt) != (1, 7):
+                nc.sync.dma_start(
+                    out=out[2 * j:2 * j + 2, P * tt:P * (tt + 1), :].rearrange("h p c -> p h c"), in_=ob[:])
 
         def prep_gate():
             nc.vector.tensor_copy(out=gate_f[0:32, :], in_=gate_bf[:])
@@ -208,37 +219,47 @@ def tile_capsule_pose_gradient_e4_kernel(tc, g_words, g_scales, w, e, d, gate, o
                 recon(j, tt)
                 finish(j, tt, vector)
 
+        dummy = accp.tile([P, 512], F32, name="acc")
+
+        def warm_up(n):
+            for i in range(n):
+                nc.tensor.matmul_mx(out=dummy[:], lhsT=zc[:, 0:P].bitcast(E4M3X4), lhsT_scale=zs[:, 0:P],
+                                    rhs=zc[:].bitcast(E4M3X4), rhs_scale=zs[:], start=True, stop=True)
+
+        warm_up(4)
         turn("w", 0)
+        warm_up(3)
         quantise("w", 0, "sv")
-        run_votes(0, (0, 1, 2, 3))
+        reorder("w", 1)
         reorder("e", 0)
-        reorder("d", 0)
+        run_votes(0, (0, 1, 2, 3))
         turn("w", 1)
-        turn("e", 0)
+        reorder("d", 0)
         quantise("w", 1, "ss")
-        reorder("d", 1)
+        turn("e", 0)
         turn("d", 0)
         quantise("e", 0, "ss")
-        turn("d", 1)
+        reorder("d", 1)
         quantise("d", 0, "ss")
-        reorder("e", 1)
-        quantise("d", 1, "vs")
         run_votes(1, (0, 1))
-        turn("e", 1)
+        turn("d", 1)
         prep_gate()
-        quantise("e", 1, "sv")
+        reorder("e", 1)
+        quantise("d", 1, "sv")
         run_votes(1, (2, 3))
+        turn("e", 1)
+        quantise("e", 1, "sv")
         reorder("e", 2)
-        run_recon(0, (0, 1), True)
+        run_recon(0, (0, 1), False)
         reorder("e", 3)
-        run_recon(0, (2, 3), True)
-        for first, second, i, tts in (("e", "w", 0, (4, 5, 6, 7)), ("w", "d", 1, (4, 5, 6, 7))):
+        run_recon(0, (2, 3), False)
+        for first, second, i, engines in (("e", "w", 0, "sv"), ("w", "d", 1, "ss")):
             for b in (2, 3):
                 turn(first, b)
                 reorder(second, b)
             for b in (2, 3):
-                quantise(first, b, "ss")
-            run_votes(i, tts)
+                quantise(first, b, engines)
+            run_votes(i, (4, 5, 6, 7))
         for b in (2, 3):
             turn("d", b)
         for b in (2, 3):

@@ -80,9 +80,11 @@ def tile_capsule_pose_gradient_e4_kernel(tc, g_words, g_scales, w, e, d, gate, o
 
         planes32 = [plane[j][:].bitcast(I32) for j in range(2)]
         nc.vector.memset(planes32[0][:, :, 0:128], 0)
+        nc.vector.memset(planes32[0][:, :, 256:384], 0)
         nc.vector.memset(zeros[:].bitcast(I32), 0)
         nc.vector.quantize_mx(out=zc[:].bitcast(E4M3X4), scales=zs[:], in_=zeros[:])
-        nc.vector.memset(planes32[0][:, :, 128:512], 0)
+        nc.vector.memset(planes32[0][:, :, 128:256], 0)
+        nc.vector.memset(planes32[0][:, :, 384:512], 0)
         nc.vector.memset(warm[:], 0.0)
         nc.vector.memset(gate_f[:], 0.0)
         nc.vector.memset(planes32[1], 0)
@@ -92,16 +94,18 @@ def tile_capsule_pose_gradient_e4_kernel(tc, g_words, g_scales, w, e, d, gate, o
             nc.gpsimd.memset(ws[j][:].bitcast(I32)[:, :, 64:128], 0)
         load_halves("w", 0)
         load_scales(nc.scalar, 0, 0, 512)
+        load_scales(nc.scalar, 0, 1024, 1536)
         nc.scalar.activation(out=warm[:], in_=warm[:], func=COPY, scale=1.0)
         load_g(0, 0)
         load("w", 1)
         load("e", 0)
-        load_scales(nc.sync, 0, 512, 2048)
         load_g(1, 0)
         load("d", 0)
         load("d", 1)
         nc.sync.dma_start(out=gate_bf[:], in_=gate.rearrange("i (t p) -> (i t) p", p=P))
         load("e", 1)
+        load_scales(nc.sync, 0, 512, 1024)
+        load_scales(nc.sync, 0, 1536, 2048)
         load_g(0, 1)
         load_g(1, 1)
         load("e", 2)
@@ -229,7 +233,7 @@ def tile_capsule_pose_gradient_e4_kernel(tc, g_words, g_scales, w, e, d, gate, o
         warm_up(4)
         turn("w", 0)
         warm_up(3)
-        quantise("w", 0, "sv")
+        quantise("w", 0, "ss")
         reorder("w", 1)
         reorder("e", 0)
         run_votes(0, (0, 1, 2, 3))

@@ -93,14 +93,14 @@ def tile_capsule_pose_gradient_e4_kernel(tc, g_words, g_scales, w, e, d, gate, o
             nc.gpsimd.memset(wc[j][:, :, 256:512], 0)
             nc.gpsimd.memset(ws[j][:].bitcast(I32)[:, :, 64:128], 0)
         load_halves("w", 0)
-        load_scales(nc.scalar, 0, 0, 512)
-        load_scales(nc.scalar, 0, 1024, 1536)
+        load_scales(nc.sync, 0, 0, 512)
         nc.scalar.activation(out=warm[:], in_=warm[:], func=COPY, scale=1.0)
         load_g(0, 0)
         load("w", 1)
         load("e", 0)
-        load_g(1, 0)
         load("d", 0)
+        load_scales(nc.sync, 0, 1024, 1536)
+        load_g(1, 0)
         load("d", 1)
         nc.sync.dma_start(out=gate_bf[:], in_=gate.rearrange("i (t p) -> (i t) p", p=P))
         load("e", 1)
@@ -234,17 +234,18 @@ def tile_capsule_pose_gradient_e4_kernel(tc, g_words, g_scales, w, e, d, gate, o
         turn("w", 0)
         warm_up(3)
         quantise("w", 0, "ss")
+        run_votes(0, (0, 1))
         reorder("w", 1)
-        reorder("e", 0)
-        run_votes(0, (0, 1, 2, 3))
         turn("w", 1)
-        reorder("d", 0)
+        reorder("e", 0)
         quantise("w", 1, "ss")
+        run_votes(0, (2, 3))
+        reorder("d", 0)
         turn("e", 0)
-        turn("d", 0)
         quantise("e", 0, "ss")
+        turn("d", 0)
         reorder("d", 1)
-        quantise("d", 0, "ss")
+        quantise("d", 0, "sv")
         run_votes(1, (0, 1))
         turn("d", 1)
         prep_gate()
@@ -257,12 +258,12 @@ def tile_capsule_pose_gradient_e4_kernel(tc, g_words, g_scales, w, e, d, gate, o
         run_recon(0, (0, 1), False)
         reorder("e", 3)
         run_recon(0, (2, 3), False)
-        for first, second, i, engines in (("e", "w", 0, "sv"), ("w", "d", 1, "ss")):
+        for first, second, i, engines in (("e", "w", 0, ("sv", "ss")), ("w", "d", 1, ("ss", "ss"))):
             for b in (2, 3):
                 turn(first, b)
                 reorder(second, b)
             for b in (2, 3):
-                quantise(first, b, engines)
+                quantise(first, b, engines[b - 2])
             run_votes(i, (4, 5, 6, 7))
         for b in (2, 3):
             turn("d", b)

@@ -53,10 +53,6 @@ def tile_capsule_pose_gradient_e4_kernel(tc, g_words, g_scales, w, e, d, gate, o
         gate_bf = keep.tile([32, P], BF16, name="gate_bf")
         gate_f = keep.tile([P, P], F32, name="gate_f")
         gate_t = keep.tile([P, 32], F32, name="gate_t")
-        zeros = keep.tile([P, 2048], BF16, name="zeros", align_bytes=64)
-        zc = keep.tile([P, 512], U32, name="zc", align_bytes=64)
-        zs = keep.tile([P, 512], U8, name="zs", align_bytes=64)
-        warm = keep.tile([P, 1], F32, name="warm")
 
         def load(kind, b):
             nc.sync.dma_start(out=raw[kind, b][:], in_=src[kind][b])
@@ -72,51 +68,44 @@ def tile_capsule_pose_gradient_e4_kernel(tc, g_words, g_scales, w, e, d, gate, o
                 out=gw[i, h][:].bitcast(I32),
                 in_=g_words.rearrange("g p n t -> p g (n t)")[:, :, 4 * n0:4 * (n0 + 512)].bitcast(I32))
 
-        def load_scales(queue, j, c0, c1):
-            for q in range(4):
-                queue.dma_start(
-                    out=plane[j][32 * q:32 * q + 4, :, c0:c1].bitcast(I32),
-                    in_=g_scales[:, 4 * q:4 * q + 4, 2048 * j + c0:2048 * j + c1].rearrange("g q n -> q g n").bitcast(I32))
+        def load_scales(j, c0, c1):
+            for r in range(4):
+                nc.sync.dma_start(
+                    out=plane[j][r:P:32, :, c0:c1].bitcast(I32),
+                    in_=g_scales[:, r:16:4, 2048 * j + c0:2048 * j + c1].rearrange("g q n -> q g n").bitcast(I32))
 
-        planes32 = [plane[j][:].bitcast(I32) for j in range(2)]
-        nc.vector.memset(planes32[0][:, :, 0:128], 0)
-        nc.vector.memset(planes32[0][:, :, 256:384], 0)
-        nc.vector.memset(zeros[:].bitcast(I32), 0)
-        nc.vector.quantize_mx(out=zc[:].bitcast(E4M3X4), scales=zs[:], in_=zeros[:])
-        nc.vector.memset(planes32[0][:, :, 128:256], 0)
-        nc.vector.memset(planes32[0][:, :, 384:512], 0)
-        nc.vector.memset(warm[:], 0.0)
+        nc.scalar.dma_start(out=gate_bf[:], in_=gate.rearrange("i (t p) -> (i t) p", p=P))
+        nc.vector.memset(plane[0][:].bitcast(I32), 0)
         nc.vector.memset(gate_f[:], 0.0)
-        nc.vector.memset(planes32[1], 0)
+        nc.vector.memset(plane[1][:].bitcast(I32), 0)
+        nc.scalar.copy(out=gate_f[0:32, :], in_=gate_bf[:])
         make_identity(nc, ident[:])
         for j in range(2):
             nc.gpsimd.memset(wc[j][:, :, 256:512], 0)
             nc.gpsimd.memset(ws[j][:].bitcast(I32)[:, :, 64:128], 0)
         load_halves("w", 0)
-        load_scales(nc.sync, 0, 0, 512)
-        nc.scalar.activation(out=warm[:], in_=warm[:], func=COPY, scale=1.0)
+        load_scales(0, 0, 1024)
         load_g(0, 0)
         load("w", 1)
         load("e", 0)
         load("d", 0)
-        load_scales(nc.sync, 0, 1024, 1536)
+        load_scales(0, 1024, 2048)
         load_g(1, 0)
         load("d", 1)
-        nc.sync.dma_start(out=gate_bf[:], in_=gate.rearrange("i (t p) -> (i t) p", p=P))
         load("e", 1)
-        load_scales(nc.sync, 0, 512, 1024)
-        load_scales(nc.sync, 0, 1536, 2048)
         load_g(0, 1)
         load_g(1, 1)
         load("e", 2)
         load("e", 3)
         load("w", 2)
         load("w", 3)
-        load_scales(nc.sync, 1, 0, 2048)
         load("d", 2)
         load("d", 3)
-        for i, h in ((2, 0), (3, 0), (2, 1), (3, 1)):
-            load_g(i, h)
+        load_g(2, 0)
+        load_g(3, 0)
+        load_scales(1, 0, 2048)
+        load_g(2, 1)
+        load_g(3, 1)
 
         ordered = {}
 
@@ -209,7 +198,6 @@ def tile_capsule_pose_gradient_e4_kernel(tc, g_words, g_scales, w, e, d, gate, o
                     out=out[2 * j:2 * j + 2, P * tt:P * (tt + 1), :].rearrange("h p c -> p h c"), in_=ob[:])
 
         def prep_gate():
-            nc.vector.tensor_copy(out=gate_f[0:32, :], in_=gate_bf[:])
             gt = xtp.tile([P, 2, 2, P], F32, name="xt")
             nc.tensor.transpose(gt[:, 0, 0, :], gate_f[:], ident[:])
             nc.vector.tensor_copy(out=gate_t[:], in_=gt[:, 0, 0, 0:32])
@@ -223,16 +211,8 @@ def tile_capsule_pose_gradient_e4_kernel(tc, g_words, g_scales, w, e, d, gate, o
                 recon(j, tt)
                 finish(j, tt, vector)
 
-        dummy = accp.tile([P, 512], F32, name="acc")
-
-        def warm_up(n):
-            for i in range(n):
-                nc.tensor.matmul_mx(out=dummy[:], lhsT=zc[:, 0:P].bitcast(E4M3X4), lhsT_scale=zs[:, 0:P],
-                                    rhs=zc[:].bitcast(E4M3X4), rhs_scale=zs[:], start=True, stop=True)
-
-        warm_up(4)
         turn("w", 0)
-        warm_up(3)
+        prep_gate()
         quantise("w", 0, "ss")
         run_votes(0, (0, 1))
         reorder("w", 1)
@@ -248,7 +228,6 @@ def tile_capsule_pose_gradient_e4_kernel(tc, g_words, g_scales, w, e, d, gate, o
         quantise("d", 0, "sv")
         run_votes(1, (0, 1))
         turn("d", 1)
-        prep_gate()
         reorder("e", 1)
         quantise("d", 1, "sv")
         run_votes(1, (2, 3))

from contextlib import ExitStack

import concourse.mybir as mybir
from concourse.masks import make_identity

F32 = mybir.dt.float32
BF16 = mybir.dt.bfloat16
U32 = mybir.dt.uint32
I32 = mybir.dt.int32
U8 = mybir.dt.uint8
E4M3X4 = mybir.dt.float8_e4m3fn_x4
E5M2X4 = mybir.dt.float8_e5m2_x4
COPY = mybir.ActivationFunctionType.Copy
MULT = mybir.AluOpType.mult

TYPES, TOKENS, POSE, K = 4, 1024, 256, 1024
P = 128
G = K // 512

FLOPS = 2 * TYPES * TOKENS * POSE * (K + K)
BYTES = 2 * 128 * 4096 * 4 + 2 * 16 * 4096 + 3 * 2 * 1024 * 1024 + 2 * 4096 + 4 * 4096 * 256


def tile_capsule_pose_gradient_e4_kernel(tc, g_words, g_scales, w, e, d, gate, out):
    nc = tc.nc
    with ExitStack() as ctx:
        keep = ctx.enter_context(tc.tile_pool(name="keep", bufs=1))
        stage = ctx.enter_context(tc.tile_pool(name="stage", bufs=3))
        outs = ctx.enter_context(tc.tile_pool(name="outs", bufs=8))
        xtp = ctx.enter_context(tc.psum_pool(name="xtp", bufs=4))
        accp = ctx.enter_context(tc.psum_pool(name="accp", bufs=4))
        ctx.enter_context(tc.manual_schedule())

        raw = {}
        for kind, n in (("w", 4), ("d", 4), ("e", 4)):
            for b in range(n):
                raw[kind, b] = keep.tile([P, 2, K], BF16, name="raw_%s%d" % (kind, b), align_bytes=64)
        src = {"w": w.rearrange("i (p s) k -> i p s k", s=2),
               "d": d.rearrange("i (p s) k -> i p s k", s=2),
               "e": e.rearrange("(i p s) k -> i p s k", p=P, s=2)}
        gw = {}
        for i in range(TYPES):
            for h in range(2):
                gw[i, h] = keep.tile([P, G, 512], U32, name="gw_%d%d" % (i, h), align_bytes=64)
        plane = [keep.tile([P, G, 2048], U8, name="plane_%d" % j, align_bytes=64) for j in range(2)]
        wc = [keep.tile([P, G, 768], U32, name="wc_%d" % j, align_bytes=64) for j in range(2)]
        ws = [keep.tile([P, G, 768], U8, name="ws_%d" % j, align_bytes=64) for j in range(2)]
        dc = [keep.tile([P, G, 512], U32, name="dc_%d" % j, align_bytes=64) for j in range(2)]
        ds = [keep.tile([P, G, 512], U8, name="ds_%d" % j, align_bytes=64) for j in range(2)]
        ec = [keep.tile([P, G, 256], U32, name="ec_%d" % b, align_bytes=64) for b in range(4)]
        es = [keep.tile([P, G, 256], U8, name="es_%d" % b, align_bytes=64) for b in range(4)]
        ident = keep.tile([P, P], F32, name="ident")
        gate_bf = keep.tile([32, P], BF16, name="gate_bf")
        gate_f = keep.tile([P, P], F32, name="gate_f")
        gate_t = keep.tile([P, 32], F32, name="gate_t")

        def load(kind, b):
            nc.sync.dma_start(out=raw[kind, b][:], in_=src[kind][b])

        def load_halves(kind, b):
            for g in range(G):
                ks = slice(512 * g, 512 * (g + 1))
                nc.sync.dma_start(out=raw[kind, b][:, :, ks], in_=src[kind][b][:, :, ks])

        def load_g(i, h):
            n0 = TOKENS * i + 512 * h
            nc.sync.dma_start(
                out=gw[i, h][:].bitcast(I32),
                in_=g_words.rearrange("g p n t -> p g (n t)")[:, :, 4 * n0:4 * (n0 + 512)].bitcast(I32))

        def load_scales(j, c0, c1):
            for r in range(4):
                nc.sync.dma_start(
                    out=plane[j][r:P:32, :, c0:c1].bitcast(I32),
                    in_=g_scales[:, r:16:4, 2048 * j + c0:2048 * j + c1].rearrange("g q n -> q g n").bitcast(I32))

        nc.scalar.dma_start(out=gate_bf[:], in_=gate.rearrange("i (t p) -> (i t) p", p=P))
        nc.vector.memset(plane[0][:].bitcast(I32), 0)
        nc.vector.memset(gate_f[:], 0.0)
        nc.vector.memset(plane[1][:].bitcast(I32), 0)
        nc.scalar.copy(out=gate_f[0:32, :], in_=gate_bf[:])
        make_identity(nc, ident[:])
        for j in range(2):
            nc.gpsimd.memset(wc[j][:, :, 256:512], 0)
            nc.gpsimd.memset(ws[j][:].bitcast(I32)[:, :, 64:128], 0)
        load_halves("w", 0)
        load_scales(0, 0, 1024)
        load_g(0, 0)
        load("w", 1)
        load("e", 0)
        load("d", 0)
        load_scales(0, 1024, 2048)
        load_g(1, 0)
        load("d", 1)
        load("e", 1)
        load_g(0, 1)
        load_g(1, 1)
        load("e", 2)
        load("e", 3)
        load("w", 2)
        load("w", 3)
        load("d", 2)
        load("d", 3)
        load_g(2, 0)
        load_g(3, 0)
        load_scales(1, 0, 2048)
        load_g(2, 1)
        load_g(3, 1)

        ordered = {}

        def reorder(kind, b):
            t = stage.tile([P, 2, G, 2, P], F32, name="ordered", align_bytes=64)
            nc.vector.tensor_copy(
                out=t[:].rearrange("p s g u m -> p (s g) u m"),
                in_=raw[kind, b][:].rearrange("p s k -> p (s k)").bitcast(F32).rearrange(
                    "p (s m u) -> p s u m", s=4, u=2))
            ordered[kind, b] = t

        banks_of = {}

        def turn(kind, b):
            banks = []
            for g in range(G):
                xt = xtp.tile([P, 2, 2, P], F32, name="xt")
                for s in range(2):
                    for u in range(2):
                        if (kind, b) in ordered:
                            words = ordered[kind, b][:, s, g, u, :]
                        else:
                            words = raw[kind, b][:, s, :].bitcast(F32)[:, 256 * g + u:256 * (g + 1):2]
                        nc.tensor.transpose(xt[:, s, u, :], words, ident[:])
                banks.append(xt)
            banks_of[kind, b] = banks

        def quantise(kind, b, engines):
            banks = banks_of[kind, b]
            grouped = []
            for g in range(G):
                t = stage.tile([P, 1024], BF16, name="grouped%d" % g, align_bytes=64)
                dst = t[:].bitcast(F32).rearrange("p (r s u) -> p r s u", s=2, u=2)
                view = banks[g][:].rearrange("p s u r -> p r s u")
                if engines[g] == "s":
                    nc.scalar.copy(out=dst, in_=view)
                else:
                    nc.vector.tensor_copy(out=dst, in_=view)
                grouped.append(t)
            for g in range(G):
                if kind == "w":
                    c0 = 512 * (b % 2)
                    codes, scales = wc[b // 2][:, g, c0:c0 + 256], ws[b // 2][:, g, c0:c0 + 256]
                elif kind == "d":
                    c0 = 256 * (b % 2)
                    codes, scales = dc[b // 2][:, g, c0:c0 + 256], ds[b // 2][:, g, c0:c0 + 256]
                else:
                    codes, scales = ec[b][:, g, :], es[b][:, g, :]
                nc.vector.quantize_mx(out=codes.bitcast(E4M3X4), scales=scales, in_=grouped[g][:])

        acc = {}

        def votes(i, tt):
            j, h = i // 2, i % 2
            if h == 0:
                acc[j, tt] = accp.tile([P, 512], F32, name="acc")
            cols = slice(128 * (tt % 4), 128 * (tt % 4) + 128)
            n0 = TOKENS * h + 128 * tt
            mov = slice(256 * h, 256 * h + 512)
            for g in range(G):
                nc.tensor.matmul_mx(
                    out=acc[j, tt][:],
                    lhsT=gw[i, tt // 4][:, g, cols].bitcast(E5M2X4),
                    lhsT_scale=plane[j][:, g, n0:n0 + 128],
                    rhs=wc[j][:, g, mov].bitcast(E4M3X4), rhs_scale=ws[j][:, g, mov],
                    start=(h == 0 and g == 0), stop=False)

        def recon(j, tt):
            cols = slice(128 * (tt % 2), 128 * (tt % 2) + 128)
            for g in range(G):
                nc.tensor.matmul_mx(
                    out=acc[j, tt][:],
                    lhsT=ec[tt // 2][:, g, cols].bitcast(E4M3X4), lhsT_scale=es[tt // 2][:, g, cols],
                    rhs=dc[j][:, g, :].bitcast(E4M3X4), rhs_scale=ds[j][:, g, :],
                    start=False, stop=(g == G - 1))

        def finish(j, tt, vector):
            ob = outs.tile([P, 2, POSE], F32, name="ob")
            for h in range(2):
                c = (2 * j + h) * 8 + tt
                part = acc[j, tt][:, POSE * h:POSE * (h + 1)]
                if vector:
                    nc.vector.tensor_scalar(out=ob[:, h, :], in0=part, scalar1=gate_t[:, c:c + 1], scalar2=None, op0=MULT)
                else:
                    nc.scalar.activation(out=ob[:, h, :], in_=part, func=COPY, scale=gate_t[:, c:c + 1])
                if (j, tt) == (1, 7):
                    (nc.sync, nc.scalar)[h].dma_start(out=out[2 * j + h, P * tt:P * (tt + 1), :], in_=ob[:, h, :])
            if (j, tt) != (1, 7):
                nc.sync.dma_start(
                    out=out[2 * j:2 * j + 2, P * tt:P * (tt + 1), :].rearrange("h p c -> p h c"), in_=ob[:])

        def prep_gate():
            gt = xtp.tile([P, 2, 2, P], F32, name="xt")
            nc.tensor.transpose(gt[:, 0, 0, :], gate_f[:], ident[:])
            nc.vector.tensor_copy(out=gate_t[:], in_=gt[:, 0, 0, 0:32])

        def run_votes(i, tts):
            for tt in tts:
                votes(i, tt)

        def run_recon(j, tts, vector):
            for tt in tts:
                recon(j, tt)
                finish(j, tt, vector)

        turn("w", 0)
        prep_gate()
        quantise("w", 0, "ss")
        run_votes(0, (0, 1))
        reorder("w", 1)
        turn("w", 1)
        reorder("e", 0)
        quantise("w", 1, "ss")
        run_votes(0, (2, 3))
        reorder("d", 0)
        turn("e", 0)
        quantise("e", 0, "ss")
        turn("d", 0)
        reorder("d", 1)
        quantise("d", 0, "sv")
        run_votes(1, (0, 1))
        turn("d", 1)
        reorder("e", 1)
        quantise("d", 1, "sv")
        run_votes(1, (2, 3))
        turn("e", 1)
        quantise("e", 1, "sv")
        reorder("e", 2)
        run_recon(0, (0, 1), False)
        reorder("e", 3)
        run_recon(0, (2, 3), False)
        for first, second, i, engines in (("e", "w", 0, ("sv", "ss")), ("w", "d", 1, ("ss", "ss"))):
            for b in (2, 3):
                turn(first, b)
                reorder(second, b)
            for b in (2, 3):
                quantise(first, b, engines[b - 2])
            run_votes(i, (4, 5, 6, 7))
        for b in (2, 3):
            turn("d", b)
        for b in (2, 3):
            quantise("d", b, "sv")
        run_recon(0, (4, 5, 6, 7), False)
        for tt in range(8):
            votes(2, tt)
            votes(3, tt)
            run_recon(1, (tt,), tt % 2 == 0)
